import numpy as np
import ml_dtypes


def mxq(x, axis, fmt="e4m3"):
    dtype, down = {"e4m3": (ml_dtypes.float8_e4m3fn, 7), "e5m2": (ml_dtypes.float8_e5m2, 14)}[fmt]
    v = np.moveaxis(np.asarray(x, np.float32).astype(ml_dtypes.bfloat16).astype(np.float64), axis, -1)
    blocks = v.reshape(v.shape[:-1] + (-1, 32))
    amax = np.abs(blocks).max(-1, keepdims=True)
    byte = np.maximum(np.where(amax > 0, np.frexp(amax)[1] - 1 + 127, 0) - down, 1)
    scale = np.exp2(byte - 127.0)
    codes = (blocks / scale).astype(np.float32).astype(dtype).astype(np.float64)
    return np.moveaxis((codes * scale).reshape(v.shape), -1, axis)


WIDE = False


def mx_kscale(k):
    if not WIDE:
        return np.ones(k)
    levels = np.array([10, -10, 5, -5, 0])
    if k % 512:
        return np.exp2(np.random.permutation(np.resize(levels, k // 32))).repeat(32)
    a = np.empty((k // 512, 16))
    for p in range(k // 512):
        a[p, :8] = np.random.permutation(np.resize(levels, 8))
        for g in range(8):
            far = levels[np.abs(levels - a[p, g]) >= 10]
            a[p, g + 8] = far[np.random.randint(len(far))]
    return np.exp2(a.ravel()).repeat(32)


def f64(x):
    return np.asarray(x).astype(np.float64)


def striped(idx):
    return np.tile(np.asarray(idx).reshape(-1, 16).T, (8, 1)).astype(np.uint16)


def unstriped(offs):
    return offs[:16].T.reshape(-1).astype(np.int64)


E2M1 = np.array([0.0, 0.5, 1.0, 1.5, 2.0, 3.0, 4.0, 6.0, -0.0, -0.5, -1.0, -1.5, -2.0, -3.0, -4.0, -6.0])


def pack_weight(w, fmt):
    k, n = w.shape
    w = f64(np.asarray(w, np.float32).astype(ml_dtypes.bfloat16)).reshape(k // 32, 32, n)
    amax = np.abs(w).max(1)
    if fmt == "e4m3":
        byte = np.frexp(amax)[1] - 1 + 127 - 7
    else:
        mant, ex = np.frexp(amax / 6.0)
        byte = np.where(mant > 0.5, ex, ex - 1) + 127
    byte = np.clip(np.where(amax > 0, byte, 1), 1, 254)
    scaled = (w * np.exp2(127.0 - byte)[:, None, :]).reshape(k, n).astype(np.float32)
    by_word = np.ascontiguousarray(scaled.reshape(k // 512, 128, 4, n).transpose(0, 1, 3, 2))
    if fmt == "e4m3":
        words = by_word.astype(ml_dtypes.float8_e4m3fn).view(np.uint8)
    else:
        c = by_word.astype(ml_dtypes.float4_e2m1fn).view(np.uint8) & 0xF
        words = (c[..., 0::2] | (c[..., 1::2] << 4)).reshape(k // 512, 128, 2 * n)
    return np.ascontiguousarray(words), np.ascontiguousarray(byte.astype(np.uint8).reshape(k // 512, 16, n))


def unpack_weight(words, scales, fmt):
    g, _, n = scales.shape
    words = np.ascontiguousarray(words).reshape(g, 128, n, -1)
    if fmt == "e4m3":
        vals = words.view(ml_dtypes.float8_e4m3fn).astype(np.float64)
    else:
        nib = np.empty((g, 128, n, 4), np.uint8)
        nib[..., 0::2] = words & 0xF
        nib[..., 1::2] = words >> 4
        vals = E2M1[nib]
    vals = vals * np.repeat(np.exp2(scales.astype(np.float64) - 127.0), 8, axis=1)[..., None]
    return vals.transpose(0, 1, 3, 2).reshape(g * 512, n)


D, T, I, Q, Z, M = 512, 2048, 512, 128, 1024, 2048


def setup_inputs():
    n = np.random.standard_normal
    idx = np.random.permutation(T)[:I]
    idx2 = np.random.permutation(Z)[:I]
    idx3 = np.random.permutation(Z)[:I]
    idx4 = np.random.permutation(M)[:I]
    fd = mx_kscale(D)
    keysp = pack_weight(n((D, T)) / fd[:, None], "e4m3")
    return {
        "query": (n((D, Q)) * 1.0 / np.sqrt(D) * fd[:, None]).astype(np.float32),
        "query2": (n((D, Q)) * 1.0 / np.sqrt(D) * fd[:, None]).astype(np.float32),
        "keys_words": keysp[0],
        "keys_scales": keysp[1],
        "pages": (n((D, Z)) / fd[:, None]).astype(np.float32),
        "old": (np.random.uniform(0.0, 2.0, (Q, M))).astype(np.float32),
        "fade": (np.random.uniform(0.3, 0.9, (Q, 1))).astype(np.float32),
        "offs": striped(idx),
        "offs2": striped(idx2),
        "offs3": striped(idx3),
        "offs4": striped(idx4),
    }


def reference(query, query2, keys_words, keys_scales, pages, old, fade, offs, offs2, offs3, offs4):
    idx = unstriped(offs)
    idx2 = unstriped(offs2)
    idx3 = unstriped(offs3)
    idx4 = unstriped(offs4)
    keysu = unpack_weight(keys_words, keys_scales, "e4m3")
    queryq = mxq(f64(query), 0, "e4m3")
    a = queryq.T @ keysu
    query2q = mxq(f64(query2), 0, "e4m3")
    pagesq = mxq(f64(pages), 0, "e4m3")
    h0 = query2q.T @ pagesq
    s = np.maximum(a[:, idx], h0[:, idx2]) - h0[:, idx3]
    w = np.maximum(s, 0.0)
    ws = w * 2.0
    wf = np.zeros((Q, M))
    wf[:, idx4] = ws
    y = f64(old) * f64(fade) + wf
    return y

@@ -1,0 +1,135 @@
+from contextlib import ExitStack
+
+import concourse.mybir as mybir
+
+D, T, I, Q, Z, M = 512, 2048, 512, 128, 1024, 2048
+FLOPS = 2 * D * Q * (T + Z)
+
+F32 = mybir.dt.float32
+BF16 = mybir.dt.bfloat16
+I32 = mybir.dt.int32
+U32 = mybir.dt.uint32
+U16 = mybir.dt.uint16
+U8 = mybir.dt.uint8
+FP8X4 = mybir.dt.float8_e4m3fn_x4
+ALU = mybir.AluOpType
+COPY = mybir.ActivationFunctionType.Copy
+
+P = 128
+PACK = 4
+PAGE_CHUNK = 256
+VECTOR_COLS = 160
+KEY_CHUNK = 512
+KEY_CUTS = (0, 256, 512, 1024, 1536, 1792, 2048)
+SLOT_CUTS = (0, 128, 288, 512)
+OUT_CUTS = (0, 256, 768, 1280, 1792, 2048)
+
+
+def interleave(copy, dst, src):
+    copy(out=dst.rearrange("p (c i) t -> p c t i", i=4), in_=src.rearrange("p t (c i) -> p c t i", i=4))
+
+
+def tile_attend_largestof3_counts_lean_kernel(tc, query, query2, keys_words, keys_scales, pages, old, fade,
+                                               offs, offs2, offs3, offs4, out):
+    nc = tc.nc
+    with ExitStack() as ctx:
+        sb = ctx.enter_context(tc.tile_pool(name="sb", bufs=1))
+        ps = ctx.enter_context(tc.psum_pool(name="ps", bufs=8))
+
+        def load_rows(rows, name):
+            raw = sb.tile([P, PACK, rows.shape[1]], F32, name=name)
+            nc.sync.dma_start(out=raw[:], in_=rows.rearrange("(p j) w -> p j w", j=PACK))
+            return raw
+
+        def load_list(src, name):
+            lst = sb.tile([P, I // 16], U16, name=name)
+            nc.sync.dma_start(lst[:], src)
+            return lst
+
+        def quantize(grouped, name):
+            width = grouped.shape[1]
+            codes = sb.tile([P, width], U32, name=name + "_codes", align_bytes=64)
+            scales = sb.tile([P, width], U8, name=name + "_scales", align_bytes=64)
+            nc.vector.quantize_mx(out=codes[:].bitcast(FP8X4), scales=scales[:],
+                                  in_=grouped[:].rearrange("p w j -> p (w j)"))
+            return codes, scales
+
+        key_planes = sb.tile([P, KEY_CHUNK], U8, align_bytes=64)
+        nc.vector.memset(key_planes[:].bitcast(I32), 0)
+        for quad in range(4):
+            nc.scalar.dma_start(
+                out=key_planes[32 * quad : 32 * quad + 16, :].bitcast(I32),
+                in_=keys_scales[0, 4 * quad : 4 * quad + 4, :].bitcast(I32).rearrange("r (a c) -> a r c", a=4))
+        wf = sb.tile([P, M], F32)
+        nc.vector.memset(wf[:], 0.0)
+
+        n_page_chunks = Z // PAGE_CHUNK
+        q2_raw = load_rows(query2, "q2_raw")
+        page_raw = [load_rows(pages[:, 0:PAGE_CHUNK], "page_raw0")]
+        q_raw = load_rows(query, "q_raw")
+        for c in range(1, n_page_chunks):
+            page_raw.append(load_rows(pages[:, c * PAGE_CHUNK : (c + 1) * PAGE_CHUNK], "page_raw%d" % c))
+        list3 = load_list(offs3, "list3")
+        list2 = load_list(offs2, "list2")
+        words = keys_words[0].rearrange("p n t -> p (n t)")
+        key_codes = []
+        for lo, hi in zip(KEY_CUTS, KEY_CUTS[1:]):
+            codes = sb.tile([P, hi - lo], I32, name="key_codes%d" % lo, align_bytes=64)
+            nc.sync.dma_start(out=codes[:], in_=words[:, PACK * lo : PACK * hi].bitcast(I32))
+            key_codes.append(codes)
+        list1 = load_list(offs, "list1")
+        list4 = load_list(offs4, "list4")
+        fade_sb = sb.tile([P, 1], F32)
+        nc.sync.dma_start(out=fade_sb[:], in_=fade)
+        old_sb = sb.tile([P, M], F32)
+        nc.sync.dma_start(out=old_sb[:], in_=old)
+
+        q2_grouped = sb.tile([P, Q, PACK], BF16, align_bytes=64)
+        interleave(nc.vector.tensor_copy, q2_grouped[:], q2_raw[:])
+        q2_codes, q2_scales = quantize(q2_grouped, "q2")
+
+        h0 = sb.tile([P, Z], F32)
+        for c in range(n_page_chunks):
+            grouped = sb.tile([P, PAGE_CHUNK, PACK], BF16, name="page_grouped%d" % c, align_bytes=64)
+            interleave(nc.vector.tensor_copy, grouped[:, :VECTOR_COLS, :], page_raw[c][:, :, :VECTOR_COLS])
+            interleave(nc.scalar.copy, grouped[:, VECTOR_COLS:, :], page_raw[c][:, :, VECTOR_COLS:])
+            codes, scales = quantize(grouped, "page%d" % c)
+            bank = ps.tile([P, 512], F32, name="bank")
+            nc.tensor.matmul_mx(out=bank[:, :PAGE_CHUNK], lhsT=q2_codes[:].bitcast(FP8X4), lhsT_scale=q2_scales[:],
+                                rhs=codes[:].bitcast(FP8X4), rhs_scale=scales[:], start=True, stop=True)
+            nc.scalar.copy(out=h0[:, c * PAGE_CHUNK : (c + 1) * PAGE_CHUNK], in_=bank[:, :PAGE_CHUNK])
+            if c == 0:
+                q_grouped = sb.tile([P, Q, PACK], BF16, align_bytes=64)
+                interleave(nc.scalar.copy, q_grouped[:], q_raw[:])
+                q_codes, q_scales = quantize(q_grouped, "q")
+
+        a = sb.tile([P, T], F32)
+        for codes, lo, hi in zip(key_codes, KEY_CUTS, KEY_CUTS[1:]):
+            plane, col = divmod(lo, KEY_CHUNK)
+            bank = ps.tile([P, 512], F32, name="bank")
+            nc.tensor.matmul_mx(out=bank[:, : hi - lo], lhsT=q_codes[:].bitcast(FP8X4), lhsT_scale=q_scales[:],
+                                rhs=codes[:].bitcast(FP8X4), rhs_scale=key_planes[4 * plane :, col : col + hi - lo],
+                                start=True, stop=True)
+            copy = nc.scalar.copy if hi == T else nc.vector.tensor_copy
+            copy(out=a[:, lo:hi], in_=bank[:, : hi - lo])
+
+        tags = [("less0", "second0", "floor0", "first0"), ("less1", "second1", "floor1", "first1"),
+                ("floor0", "first0", "first1", "first2")]
+        for (less_tag, second_tag, floor_tag, first_tag), lo, hi in zip(tags, SLOT_CUTS, SLOT_CUTS[1:]):
+            cols = slice(lo // 16, hi // 16)
+            less = sb.tile([P, hi - lo], F32, tag=less_tag)
+            nc.scalar.activation(less[:], h0[:].indirect(list3[:, cols]), COPY, scale=-2.0)
+            second = sb.tile([P, hi - lo], F32, tag=second_tag)
+            nc.scalar.activation(second[:], h0[:].indirect(list2[:, cols]), COPY, scale=2.0)
+            floor = sb.tile([P, hi - lo], F32, tag=floor_tag)
+            nc.vector.scalar_tensor_tensor(floor[:], less[:], -1.0, second[:], ALU.mult, ALU.max)
+            first = sb.tile([P, hi - lo], F32, tag=first_tag)
+            nc.scalar.activation(first[:], a[:].indirect(list1[:, cols]), COPY, scale=2.0)
+            largest = sb.tile([P, hi - lo], F32)
+            nc.vector.tensor_tensor(largest[:], first[:], floor[:], ALU.max)
+            nc.vector.tensor_tensor(wf[:].indirect(list4[:, cols]), largest[:], less[:], ALU.add)
+
+        for lo, hi in zip(OUT_CUTS, OUT_CUTS[1:]):
+            res = sb.tile([P, hi - lo], F32, name="res%d" % lo)
+            nc.vector.scalar_tensor_tensor(res[:], old_sb[:, lo:hi], fade_sb[:], wf[:, lo:hi], ALU.mult, ALU.add)
+            nc.sync.dma_start(out=out[:, lo:hi], in_=res[:])

@@ -17,12 +17,15 @@ COPY = mybir.ActivationFunctionType.Copy
 
 P = 128
 PACK = 4
+PAGE_LOADS = (0, 256, 512, 768, 1024)
 PAGE_CHUNK = 256
 VECTOR_COLS = 160
+HALF = 128
 KEY_CHUNK = 512
-KEY_CUTS = (0, 256, 512, 1024, 1536, 1792, 2048)
-SLOT_CUTS = (0, 128, 288, 512)
-OUT_CUTS = (0, 256, 768, 1280, 1792, 2048)
+KEY_LOADS = (0, 256, 768, 1280, 1792, 2048)
+KEY_PASS = 256
+SLOT_CUTS = (128, 288)
+OUT_CUTS = (0, 128, 384, 896, 1408, 1920, 2048)
 
 
 def interleave(copy, dst, src):
@@ -34,7 +37,7 @@ def tile_attend_largestof3_counts_lean_kernel(tc, query, query2, keys_words, key
     nc = tc.nc
     with ExitStack() as ctx:
         sb = ctx.enter_context(tc.tile_pool(name="sb", bufs=1))
-        ps = ctx.enter_context(tc.psum_pool(name="ps", bufs=8))
+        ps = ctx.enter_context(tc.psum_pool(name="ps", bufs=1))
 
         def load_rows(rows, name):
             raw = sb.tile([P, PACK, rows.shape[1]], F32, name=name)
@@ -51,32 +54,31 @@ def tile_attend_largestof3_counts_lean_kernel(tc, query, query2, keys_words, key
             codes = sb.tile([P, width], U32, name=name + "_codes", align_bytes=64)
             scales = sb.tile([P, width], U8, name=name + "_scales", align_bytes=64)
             nc.vector.quantize_mx(out=codes[:].bitcast(FP8X4), scales=scales[:],
-                                  in_=grouped[:].rearrange("p w j -> p (w j)"))
+                                  in_=grouped.rearrange("p w j -> p (w j)"))
             return codes, scales
 
         key_planes = sb.tile([P, KEY_CHUNK], U8, align_bytes=64)
         nc.vector.memset(key_planes[:].bitcast(I32), 0)
-        for quad in range(4):
-            nc.scalar.dma_start(
-                out=key_planes[32 * quad : 32 * quad + 16, :].bitcast(I32),
-                in_=keys_scales[0, 4 * quad : 4 * quad + 4, :].bitcast(I32).rearrange("r (a c) -> a r c", a=4))
         wf = sb.tile([P, M], F32)
         nc.vector.memset(wf[:], 0.0)
 
-        n_page_chunks = Z // PAGE_CHUNK
         q2_raw = load_rows(query2, "q2_raw")
-        page_raw = [load_rows(pages[:, 0:PAGE_CHUNK], "page_raw0")]
         q_raw = load_rows(query, "q_raw")
-        for c in range(1, n_page_chunks):
-            page_raw.append(load_rows(pages[:, c * PAGE_CHUNK : (c + 1) * PAGE_CHUNK], "page_raw%d" % c))
-        list3 = load_list(offs3, "list3")
-        list2 = load_list(offs2, "list2")
+        scale_rows = sb.tile([P, KEY_CHUNK // 4], I32)
+        for quad in range(4):
+            nc.sync.dma_start(
+                out=scale_rows[32 * quad : 32 * quad + 16, :],
+                in_=keys_scales[0, 4 * quad : 4 * quad + 4, :].bitcast(I32).rearrange("r (a c) -> a r c", a=4))
+        page_raw = [load_rows(pages[:, lo:hi], "page_raw%d" % lo) for lo, hi in zip(PAGE_LOADS, PAGE_LOADS[1:])]
         words = keys_words[0].rearrange("p n t -> p (n t)")
         key_codes = []
-        for lo, hi in zip(KEY_CUTS, KEY_CUTS[1:]):
+        for lo, hi in zip(KEY_LOADS, KEY_LOADS[1:]):
             codes = sb.tile([P, hi - lo], I32, name="key_codes%d" % lo, align_bytes=64)
             nc.sync.dma_start(out=codes[:], in_=words[:, PACK * lo : PACK * hi].bitcast(I32))
             key_codes.append(codes)
+            if len(key_codes) == 1:
+                list3 = load_list(offs3, "list3")
+                list2 = load_list(offs2, "list2")
         list1 = load_list(offs, "list1")
         list4 = load_list(offs4, "list4")
         fade_sb = sb.tile([P, 1], F32)
@@ -86,48 +88,87 @@ def tile_attend_largestof3_counts_lean_kernel(tc, query, query2, keys_words, key
 
         q2_grouped = sb.tile([P, Q, PACK], BF16, align_bytes=64)
         interleave(nc.vector.tensor_copy, q2_grouped[:], q2_raw[:])
-        q2_codes, q2_scales = quantize(q2_grouped, "q2")
+        q2_codes, q2_scales = quantize(q2_grouped[:], "q2")
+
+        q_grouped = sb.tile([P, Q, PACK], BF16, align_bytes=64)
+        interleave(nc.scalar.copy, q_grouped[:], q_raw[:])
+        q_codes, q_scales = quantize(q_grouped[:], "q")
+
+        for quad in range(4):
+            rows = slice(32 * quad, 32 * quad + 16)
+            nc.vector.tensor_copy(out=key_planes[rows, :].bitcast(I32), in_=scale_rows[rows, :])
 
         h0 = sb.tile([P, Z], F32)
-        for c in range(n_page_chunks):
-            grouped = sb.tile([P, PAGE_CHUNK, PACK], BF16, name="page_grouped%d" % c, align_bytes=64)
-            interleave(nc.vector.tensor_copy, grouped[:, :VECTOR_COLS, :], page_raw[c][:, :, :VECTOR_COLS])
-            interleave(nc.scalar.copy, grouped[:, VECTOR_COLS:, :], page_raw[c][:, :, VECTOR_COLS:])
-            codes, scales = quantize(grouped, "page%d" % c)
-            bank = ps.tile([P, 512], F32, name="bank")
-            nc.tensor.matmul_mx(out=bank[:, :PAGE_CHUNK], lhsT=q2_codes[:].bitcast(FP8X4), lhsT_scale=q2_scales[:],
-                                rhs=codes[:].bitcast(FP8X4), rhs_scale=scales[:], start=True, stop=True)
-            nc.scalar.copy(out=h0[:, c * PAGE_CHUNK : (c + 1) * PAGE_CHUNK], in_=bank[:, :PAGE_CHUNK])
-            if c == 0:
-                q_grouped = sb.tile([P, Q, PACK], BF16, align_bytes=64)
-                interleave(nc.scalar.copy, q_grouped[:], q_raw[:])
-                q_codes, q_scales = quantize(q_grouped, "q")
 
-        a = sb.tile([P, T], F32)
-        for codes, lo, hi in zip(key_codes, KEY_CUTS, KEY_CUTS[1:]):
-            plane, col = divmod(lo, KEY_CHUNK)
-            bank = ps.tile([P, 512], F32, name="bank")
-            nc.tensor.matmul_mx(out=bank[:, : hi - lo], lhsT=q_codes[:].bitcast(FP8X4), lhsT_scale=q_scales[:],
-                                rhs=codes[:].bitcast(FP8X4), rhs_scale=key_planes[4 * plane :, col : col + hi - lo],
-                                start=True, stop=True)
+        def score_pages(grouped, lo, copy):
+            width = grouped.shape[1]
+            codes, scales = quantize(grouped, "page%d" % lo)
+            bank = ps.tile([P, 512], F32, tag="bank%d" % lo)
+            nc.tensor.matmul_mx(out=bank[:, :width], lhsT=q2_codes[:].bitcast(FP8X4), lhsT_scale=q2_scales[:],
+                                rhs=codes[:].bitcast(FP8X4), rhs_scale=scales[:], start=True, stop=True)
+            copy(out=h0[:, lo : lo + width], in_=bank[:, :width])
+
+        for lo in range(0, Z, PAGE_CHUNK):
+            load = max(n for n, start in enumerate(PAGE_LOADS) if start <= lo)
+            raw = page_raw[load][:, :, lo - PAGE_LOADS[load] : lo - PAGE_LOADS[load] + PAGE_CHUNK]
+            grouped = sb.tile([P, PAGE_CHUNK, PACK], BF16, name="page_grouped%d" % lo, align_bytes=64)
+            last = lo + PAGE_CHUNK == Z
+            for a0, a1 in ((0, HALF), (HALF, VECTOR_COLS)) if last else ((0, VECTOR_COLS),):
+                interleave(nc.vector.tensor_copy, grouped[:, a0:a1, :], raw[:, :, a0:a1])
+            interleave(nc.scalar.copy, grouped[:, VECTOR_COLS:, :], raw[:, :, VECTOR_COLS:])
+            if last:
+                score_pages(grouped[:, :HALF, :], lo, nc.scalar.copy)
+                score_pages(grouped[:, HALF:, :], lo + HALF, nc.scalar.copy)
+            else:
+                score_pages(grouped[:], lo, nc.scalar.copy)
+
+        a = sb.tile([P, T], F32, tag="page_raw768")
+        for codes, lo, hi, tag in zip(key_codes, KEY_LOADS, KEY_LOADS[1:], (256, 256, 768, 896, 256)):
+            bank = ps.tile([P, 512], F32, tag="bank%d" % tag)
+            for start in range(lo, hi, KEY_PASS):
+                plane, col = divmod(start, KEY_CHUNK)
+                cols = slice(start - lo, start - lo + KEY_PASS)
+                nc.tensor.matmul_mx(out=bank[:, cols], lhsT=q_codes[:].bitcast(FP8X4), lhsT_scale=q_scales[:],
+                                    rhs=codes[:, cols].bitcast(FP8X4),
+                                    rhs_scale=key_planes[4 * plane :, col : col + KEY_PASS], start=True, stop=True)
             copy = nc.scalar.copy if hi == T else nc.vector.tensor_copy
             copy(out=a[:, lo:hi], in_=bank[:, : hi - lo])
 
-        tags = [("less0", "second0", "floor0", "first0"), ("less1", "second1", "floor1", "first1"),
-                ("floor0", "first0", "first1", "first2")]
-        for (less_tag, second_tag, floor_tag, first_tag), lo, hi in zip(tags, SLOT_CUTS, SLOT_CUTS[1:]):
-            cols = slice(lo // 16, hi // 16)
-            less = sb.tile([P, hi - lo], F32, tag=less_tag)
-            nc.scalar.activation(less[:], h0[:].indirect(list3[:, cols]), COPY, scale=-2.0)
-            second = sb.tile([P, hi - lo], F32, tag=second_tag)
-            nc.scalar.activation(second[:], h0[:].indirect(list2[:, cols]), COPY, scale=2.0)
-            floor = sb.tile([P, hi - lo], F32, tag=floor_tag)
-            nc.vector.scalar_tensor_tensor(floor[:], less[:], -1.0, second[:], ALU.mult, ALU.max)
-            first = sb.tile([P, hi - lo], F32, tag=first_tag)
-            nc.scalar.activation(first[:], a[:].indirect(list1[:, cols]), COPY, scale=2.0)
-            largest = sb.tile([P, hi - lo], F32)
-            nc.vector.tensor_tensor(largest[:], first[:], floor[:], ALU.max)
-            nc.vector.tensor_tensor(wf[:].indirect(list4[:, cols]), largest[:], less[:], ALU.add)
+        def listed(window, lst, lo, hi):
+            return window[:].indirect(lst[:, lo // 16 : hi // 16])
+
+        def floor_of(floor, less, second):
+            nc.vector.scalar_tensor_tensor(floor, second, -2.0, less, ALU.mult, ALU.min)
+
+        def largest_of(largest, floor, first):
+            nc.vector.scalar_tensor_tensor(largest, floor, -1.0, first, ALU.mult, ALU.max)
+
+        s1, s2 = SLOT_CUTS
+        early, late = s2, I - s2
+        pad = late - s1
+        less_early = sb.tile([P, early], F32)
+        second_early = sb.tile([P, early], F32)
+        floors = sb.tile([P, pad + early + late], F32, tag="key_codes%d" % KEY_LOADS[-2], align_bytes=64)
+        firsts = sb.tile([P, pad + early], F32)
+        largest = sb.tile([P, I], F32)
+        floor_early, second_late, floor_late = floors[:, pad : pad + early], floors[:, pad + early :], floors[:, :late]
+        first_early, first_late = firsts[:, pad:], firsts[:, :late]
+        less_late = second_early[:, :late]
+
+        nc.scalar.activation(less_early[:], listed(h0, list3, 0, s2), COPY, scale=-2.0)
+        nc.scalar.activation(second_early[:], listed(h0, list2, 0, s2), COPY)
+        nc.vector.tensor_copy(second_late, listed(h0, list2, s2, I))
+        floor_of(floor_early, less_early[:], second_early[:])
+        for lo, hi in ((0, s1), (s1, s2)):
+            nc.scalar.activation(first_early[:, lo:hi], listed(a, list1, lo, hi), COPY, scale=2.0)
+            largest_of(largest[:, lo:hi], floor_early[:, lo:hi], first_early[:, lo:hi])
+        nc.vector.tensor_tensor(listed(wf, list4, 0, s1), largest[:, :s1], less_early[:, :s1], ALU.add)
+        nc.scalar.activation(less_late, listed(h0, list3, s2, I), COPY, scale=-2.0)
+        nc.scalar.activation(first_late, listed(a, list1, s2, I), COPY, scale=2.0)
+        floor_of(floor_late, less_late, second_late)
+        nc.vector.tensor_tensor(listed(wf, list4, s1, s2), largest[:, s1:s2], less_early[:, s1:s2], ALU.add)
+        largest_of(largest[:, s2:], floor_late, first_late)
+        nc.vector.tensor_tensor(listed(wf, list4, s2, I), largest[:, s2:], less_late, ALU.add)
 
         for lo, hi in zip(OUT_CUTS, OUT_CUTS[1:]):
             res = sb.tile([P, hi - lo], F32, name="res%d" % lo)

@@ -17,14 +17,18 @@ COPY = mybir.ActivationFunctionType.Copy
 
 P = 128
 PACK = 4
-PAGE_LOADS = (0, 256, 512, 768, 1024)
+BANK = 512
+LIST_ROWS = 16
+
 PAGE_CHUNK = 256
-VECTOR_COLS = 160
-HALF = 128
-KEY_CHUNK = 512
-KEY_LOADS = (0, 256, 768, 1280, 1792, 2048)
+PAGE_HALF = PAGE_CHUNK // 2
+VECTOR_PAGES = 160
+
+PLANE = 512
 KEY_PASS = 256
-SLOT_CUTS = (128, 288)
+KEY_LOADS = (0, 256, 768, 1280, 1792, 2048)
+
+SLOT_CUTS = (128, 256)
 OUT_CUTS = (0, 128, 384, 896, 1408, 1920, 2048)
 
 
@@ -39,44 +43,44 @@ def tile_attend_largestof3_counts_lean_kernel(tc, query, query2, keys_words, key
         sb = ctx.enter_context(tc.tile_pool(name="sb", bufs=1))
         ps = ctx.enter_context(tc.psum_pool(name="ps", bufs=1))
 
-        def load_rows(rows, name):
-            raw = sb.tile([P, PACK, rows.shape[1]], F32, name=name)
-            nc.sync.dma_start(out=raw[:], in_=rows.rearrange("(p j) w -> p j w", j=PACK))
+        def load_features(columns, name):
+            raw = sb.tile([P, PACK, columns.shape[1]], F32, name=name)
+            nc.sync.dma_start(out=raw[:], in_=columns.rearrange("(p t) w -> p t w", t=PACK))
             return raw
 
         def load_list(src, name):
-            lst = sb.tile([P, I // 16], U16, name=name)
-            nc.sync.dma_start(lst[:], src)
-            return lst
+            offsets = sb.tile([P, I // LIST_ROWS], U16, name=name)
+            nc.sync.dma_start(offsets[:], src)
+            return offsets
 
         def quantize(grouped, name):
             width = grouped.shape[1]
             codes = sb.tile([P, width], U32, name=name + "_codes", align_bytes=64)
             scales = sb.tile([P, width], U8, name=name + "_scales", align_bytes=64)
             nc.vector.quantize_mx(out=codes[:].bitcast(FP8X4), scales=scales[:],
-                                  in_=grouped.rearrange("p w j -> p (w j)"))
+                                  in_=grouped.rearrange("p w t -> p (w t)"))
             return codes, scales
 
-        key_planes = sb.tile([P, KEY_CHUNK], U8, align_bytes=64)
+        key_planes = sb.tile([P, PLANE], U8, align_bytes=64)
         nc.vector.memset(key_planes[:].bitcast(I32), 0)
         wf = sb.tile([P, M], F32)
         nc.vector.memset(wf[:], 0.0)
 
-        q2_raw = load_rows(query2, "q2_raw")
-        q_raw = load_rows(query, "q_raw")
-        scale_rows = sb.tile([P, KEY_CHUNK // 4], I32)
-        for quad in range(4):
+        q2_raw = load_features(query2, "q2_raw")
+        q_raw = load_features(query, "q_raw")
+        scale_rows = sb.tile([P, PLANE // 4], I32)
+        for g in range(4):
             nc.sync.dma_start(
-                out=scale_rows[32 * quad : 32 * quad + 16, :],
-                in_=keys_scales[0, 4 * quad : 4 * quad + 4, :].bitcast(I32).rearrange("r (a c) -> a r c", a=4))
-        page_raw = [load_rows(pages[:, lo:hi], "page_raw%d" % lo) for lo, hi in zip(PAGE_LOADS, PAGE_LOADS[1:])]
+                out=scale_rows[32 * g : 32 * g + 16, :],
+                in_=keys_scales[0, 4 * g : 4 * g + 4, :].bitcast(I32).rearrange("r (n c) -> n r c", n=T // PLANE))
+        page_raw = [load_features(pages[:, lo : lo + PAGE_CHUNK], "page_raw%d" % lo) for lo in range(0, Z, PAGE_CHUNK)]
         words = keys_words[0].rearrange("p n t -> p (n t)")
         key_codes = []
         for lo, hi in zip(KEY_LOADS, KEY_LOADS[1:]):
             codes = sb.tile([P, hi - lo], I32, name="key_codes%d" % lo, align_bytes=64)
             nc.sync.dma_start(out=codes[:], in_=words[:, PACK * lo : PACK * hi].bitcast(I32))
             key_codes.append(codes)
-            if len(key_codes) == 1:
+            if lo == 0:
                 list3 = load_list(offs3, "list3")
                 list2 = load_list(offs2, "list2")
         list1 = load_list(offs, "list1")
@@ -94,39 +98,39 @@ def tile_attend_largestof3_counts_lean_kernel(tc, query, query2, keys_words, key
         interleave(nc.scalar.copy, q_grouped[:], q_raw[:])
         q_codes, q_scales = quantize(q_grouped[:], "q")
 
-        for quad in range(4):
-            rows = slice(32 * quad, 32 * quad + 16)
+        for g in range(4):
+            rows = slice(32 * g, 32 * g + 16)
             nc.vector.tensor_copy(out=key_planes[rows, :].bitcast(I32), in_=scale_rows[rows, :])
 
         h0 = sb.tile([P, Z], F32)
 
-        def score_pages(grouped, lo, copy):
+        def score_pages(grouped, lo):
             width = grouped.shape[1]
             codes, scales = quantize(grouped, "page%d" % lo)
-            bank = ps.tile([P, 512], F32, tag="bank%d" % lo)
+            bank = ps.tile([P, BANK], F32, tag="bank%d" % lo)
             nc.tensor.matmul_mx(out=bank[:, :width], lhsT=q2_codes[:].bitcast(FP8X4), lhsT_scale=q2_scales[:],
                                 rhs=codes[:].bitcast(FP8X4), rhs_scale=scales[:], start=True, stop=True)
-            copy(out=h0[:, lo : lo + width], in_=bank[:, :width])
+            nc.scalar.copy(out=h0[:, lo : lo + width], in_=bank[:, :width])
 
-        for lo in range(0, Z, PAGE_CHUNK):
-            load = max(n for n, start in enumerate(PAGE_LOADS) if start <= lo)
-            raw = page_raw[load][:, :, lo - PAGE_LOADS[load] : lo - PAGE_LOADS[load] + PAGE_CHUNK]
+        last_chunk = Z - PAGE_CHUNK
+        for raw, lo in zip(page_raw, range(0, Z, PAGE_CHUNK)):
             grouped = sb.tile([P, PAGE_CHUNK, PACK], BF16, name="page_grouped%d" % lo, align_bytes=64)
-            last = lo + PAGE_CHUNK == Z
-            for a0, a1 in ((0, HALF), (HALF, VECTOR_COLS)) if last else ((0, VECTOR_COLS),):
-                interleave(nc.vector.tensor_copy, grouped[:, a0:a1, :], raw[:, :, a0:a1])
-            interleave(nc.scalar.copy, grouped[:, VECTOR_COLS:, :], raw[:, :, VECTOR_COLS:])
-            if last:
-                score_pages(grouped[:, :HALF, :], lo, nc.scalar.copy)
-                score_pages(grouped[:, HALF:, :], lo + HALF, nc.scalar.copy)
+            vector_cuts = (0, PAGE_HALF, VECTOR_PAGES) if lo == last_chunk else (0, VECTOR_PAGES)
+            for c0, c1 in zip(vector_cuts, vector_cuts[1:]):
+                interleave(nc.vector.tensor_copy, grouped[:, c0:c1, :], raw[:, :, c0:c1])
+            interleave(nc.scalar.copy, grouped[:, VECTOR_PAGES:, :], raw[:, :, VECTOR_PAGES:])
+            if lo == last_chunk:
+                score_pages(grouped[:, :PAGE_HALF, :], lo)
+                score_pages(grouped[:, PAGE_HALF:, :], lo + PAGE_HALF)
             else:
-                score_pages(grouped[:], lo, nc.scalar.copy)
+                score_pages(grouped[:], lo)
 
-        a = sb.tile([P, T], F32, tag="page_raw768")
-        for codes, lo, hi, tag in zip(key_codes, KEY_LOADS, KEY_LOADS[1:], (256, 256, 768, 896, 256)):
-            bank = ps.tile([P, 512], F32, tag="bank%d" % tag)
+        a = sb.tile([P, T], F32, tag="page_raw%d" % last_chunk)
+        key_banks = (PAGE_CHUNK, PAGE_CHUNK, last_chunk, last_chunk + PAGE_HALF, PAGE_CHUNK)
+        for codes, lo, hi, page_bank in zip(key_codes, KEY_LOADS, KEY_LOADS[1:], key_banks):
+            bank = ps.tile([P, BANK], F32, tag="bank%d" % page_bank)
             for start in range(lo, hi, KEY_PASS):
-                plane, col = divmod(start, KEY_CHUNK)
+                plane, col = divmod(start, PLANE)
                 cols = slice(start - lo, start - lo + KEY_PASS)
                 nc.tensor.matmul_mx(out=bank[:, cols], lhsT=q_codes[:].bitcast(FP8X4), lhsT_scale=q_scales[:],
                                     rhs=codes[:, cols].bitcast(FP8X4),
@@ -134,8 +138,8 @@ def tile_attend_largestof3_counts_lean_kernel(tc, query, query2, keys_words, key
             copy = nc.scalar.copy if hi == T else nc.vector.tensor_copy
             copy(out=a[:, lo:hi], in_=bank[:, : hi - lo])
 
-        def listed(window, lst, lo, hi):
-            return window[:].indirect(lst[:, lo // 16 : hi // 16])
+        def listed(window, offsets, lo, hi):
+            return window[:].indirect(offsets[:, lo // LIST_ROWS : hi // LIST_ROWS])
 
         def floor_of(floor, less, second):
             nc.vector.scalar_tensor_tensor(floor, second, -2.0, less, ALU.mult, ALU.min)

from contextlib import ExitStack

import concourse.mybir as mybir

D, T, I, Q, Z, M = 512, 2048, 512, 128, 1024, 2048
FLOPS = 2 * D * Q * (T + Z)

F32 = mybir.dt.float32
BF16 = mybir.dt.bfloat16
I32 = mybir.dt.int32
U32 = mybir.dt.uint32
U16 = mybir.dt.uint16
U8 = mybir.dt.uint8
FP8X4 = mybir.dt.float8_e4m3fn_x4
ALU = mybir.AluOpType
COPY = mybir.ActivationFunctionType.Copy

P = 128
PACK = 4
BANK = 512
LIST_ROWS = 16

PAGE_CHUNK = 256
PAGE_HALF = PAGE_CHUNK // 2
VECTOR_PAGES = 160

PLANE = 512
KEY_PASS = 256
KEY_LOADS = (0, 256, 768, 1280, 1792, 2048)

SLOT_CUTS = (128, 256)
OUT_CUTS = (0, 128, 384, 896, 1408, 1920, 2048)


def interleave(copy, dst, src):
    copy(out=dst.rearrange("p (c i) t -> p c t i", i=4), in_=src.rearrange("p t (c i) -> p c t i", i=4))


def tile_attend_largestof3_counts_lean_kernel(tc, query, query2, keys_words, keys_scales, pages, old, fade,
                                               offs, offs2, offs3, offs4, out):
    nc = tc.nc
    with ExitStack() as ctx:
        sb = ctx.enter_context(tc.tile_pool(name="sb", bufs=1))
        ps = ctx.enter_context(tc.psum_pool(name="ps", bufs=1))

        def load_features(columns, name):
            raw = sb.tile([P, PACK, columns.shape[1]], F32, name=name)
            nc.sync.dma_start(out=raw[:], in_=columns.rearrange("(p t) w -> p t w", t=PACK))
            return raw

        def load_list(src, name):
            offsets = sb.tile([P, I // LIST_ROWS], U16, name=name)
            nc.sync.dma_start(offsets[:], src)
            return offsets

        def quantize(grouped, name):
            width = grouped.shape[1]
            codes = sb.tile([P, width], U32, name=name + "_codes", align_bytes=64)
            scales = sb.tile([P, width], U8, name=name + "_scales", align_bytes=64)
            nc.vector.quantize_mx(out=codes[:].bitcast(FP8X4), scales=scales[:],
                                  in_=grouped.rearrange("p w t -> p (w t)"))
            return codes, scales

        key_planes = sb.tile([P, PLANE], U8, align_bytes=64)
        nc.vector.memset(key_planes[:].bitcast(I32), 0)
        wf = sb.tile([P, M], F32)
        nc.vector.memset(wf[:], 0.0)

        q2_raw = load_features(query2, "q2_raw")
        q_raw = load_features(query, "q_raw")
        scale_rows = sb.tile([P, PLANE // 4], I32)
        for g in range(4):
            nc.sync.dma_start(
                out=scale_rows[32 * g : 32 * g + 16, :],
                in_=keys_scales[0, 4 * g : 4 * g + 4, :].bitcast(I32).rearrange("r (n c) -> n r c", n=T // PLANE))
        page_raw = [load_features(pages[:, lo : lo + PAGE_CHUNK], "page_raw%d" % lo) for lo in range(0, Z, PAGE_CHUNK)]
        words = keys_words[0].rearrange("p n t -> p (n t)")
        key_codes = []
        for lo, hi in zip(KEY_LOADS, KEY_LOADS[1:]):
            codes = sb.tile([P, hi - lo], I32, name="key_codes%d" % lo, align_bytes=64)
            nc.sync.dma_start(out=codes[:], in_=words[:, PACK * lo : PACK * hi].bitcast(I32))
            key_codes.append(codes)
            if lo == 0:
                list3 = load_list(offs3, "list3")
                list2 = load_list(offs2, "list2")
        list1 = load_list(offs, "list1")
        list4 = load_list(offs4, "list4")
        fade_sb = sb.tile([P, 1], F32)
        nc.sync.dma_start(out=fade_sb[:], in_=fade)
        old_sb = sb.tile([P, M], F32)
        nc.sync.dma_start(out=old_sb[:], in_=old)

        q2_grouped = sb.tile([P, Q, PACK], BF16, align_bytes=64)
        interleave(nc.vector.tensor_copy, q2_grouped[:], q2_raw[:])
        q2_codes, q2_scales = quantize(q2_grouped[:], "q2")

        q_grouped = sb.tile([P, Q, PACK], BF16, align_bytes=64)
        interleave(nc.scalar.copy, q_grouped[:], q_raw[:])
        q_codes, q_scales = quantize(q_grouped[:], "q")

        for g in range(4):
            rows = slice(32 * g, 32 * g + 16)
            nc.vector.tensor_copy(out=key_planes[rows, :].bitcast(I32), in_=scale_rows[rows, :])

        h0 = sb.tile([P, Z], F32)

        def score_pages(grouped, lo):
            width = grouped.shape[1]
            codes, scales = quantize(grouped, "page%d" % lo)
            bank = ps.tile([P, BANK], F32, tag="bank%d" % lo)
            nc.tensor.matmul_mx(out=bank[:, :width], lhsT=q2_codes[:].bitcast(FP8X4), lhsT_scale=q2_scales[:],
                                rhs=codes[:].bitcast(FP8X4), rhs_scale=scales[:], start=True, stop=True)
            nc.scalar.copy(out=h0[:, lo : lo + width], in_=bank[:, :width])

        last_chunk = Z - PAGE_CHUNK
        for raw, lo in zip(page_raw, range(0, Z, PAGE_CHUNK)):
            grouped = sb.tile([P, PAGE_CHUNK, PACK], BF16, name="page_grouped%d" % lo, align_bytes=64)
            vector_cuts = (0, PAGE_HALF, VECTOR_PAGES) if lo == last_chunk else (0, VECTOR_PAGES)
            for c0, c1 in zip(vector_cuts, vector_cuts[1:]):
                interleave(nc.vector.tensor_copy, grouped[:, c0:c1, :], raw[:, :, c0:c1])
            interleave(nc.scalar.copy, grouped[:, VECTOR_PAGES:, :], raw[:, :, VECTOR_PAGES:])
            if lo == last_chunk:
                score_pages(grouped[:, :PAGE_HALF, :], lo)
                score_pages(grouped[:, PAGE_HALF:, :], lo + PAGE_HALF)
            else:
                score_pages(grouped[:], lo)

        a = sb.tile([P, T], F32, tag="page_raw%d" % last_chunk)
        key_banks = (PAGE_CHUNK, PAGE_CHUNK, last_chunk, last_chunk + PAGE_HALF, PAGE_CHUNK)
        for codes, lo, hi, page_bank in zip(key_codes, KEY_LOADS, KEY_LOADS[1:], key_banks):
            bank = ps.tile([P, BANK], F32, tag="bank%d" % page_bank)
            for start in range(lo, hi, KEY_PASS):
                plane, col = divmod(start, PLANE)
                cols = slice(start - lo, start - lo + KEY_PASS)
                nc.tensor.matmul_mx(out=bank[:, cols], lhsT=q_codes[:].bitcast(FP8X4), lhsT_scale=q_scales[:],
                                    rhs=codes[:, cols].bitcast(FP8X4),
                                    rhs_scale=key_planes[4 * plane :, col : col + KEY_PASS], start=True, stop=True)
            copy = nc.scalar.copy if hi == T else nc.vector.tensor_copy
            copy(out=a[:, lo:hi], in_=bank[:, : hi - lo])

        def listed(window, offsets, lo, hi):
            return window[:].indirect(offsets[:, lo // LIST_ROWS : hi // LIST_ROWS])

        def floor_of(floor, less, second):
            nc.vector.scalar_tensor_tensor(floor, second, -2.0, less, ALU.mult, ALU.min)

        def largest_of(largest, floor, first):
            nc.vector.scalar_tensor_tensor(largest, floor, -1.0, first, ALU.mult, ALU.max)

        s1, s2 = SLOT_CUTS
        early, late = s2, I - s2
        pad = late - s1
        less_early = sb.tile([P, early], F32)
        second_early = sb.tile([P, early], F32)
        floors = sb.tile([P, pad + early + late], F32, tag="key_codes%d" % KEY_LOADS[-2], align_bytes=64)
        firsts = sb.tile([P, pad + early], F32)
        largest = sb.tile([P, I], F32)
        floor_early, second_late, floor_late = floors[:, pad : pad + early], floors[:, pad + early :], floors[:, :late]
        first_early, first_late = firsts[:, pad:], firsts[:, :late]
        less_late = second_early[:, :late]

        nc.scalar.activation(less_early[:], listed(h0, list3, 0, s2), COPY, scale=-2.0)
        nc.scalar.activation(second_early[:], listed(h0, list2, 0, s2), COPY)
        nc.vector.tensor_copy(second_late, listed(h0, list2, s2, I))
        floor_of(floor_early, less_early[:], second_early[:])
        for lo, hi in ((0, s1), (s1, s2)):
            nc.scalar.activation(first_early[:, lo:hi], listed(a, list1, lo, hi), COPY, scale=2.0)
            largest_of(largest[:, lo:hi], floor_early[:, lo:hi], first_early[:, lo:hi])
        nc.vector.tensor_tensor(listed(wf, list4, 0, s1), largest[:, :s1], less_early[:, :s1], ALU.add)
        nc.scalar.activation(less_late, listed(h0, list3, s2, I), COPY, scale=-2.0)
        nc.scalar.activation(first_late, listed(a, list1, s2, I), COPY, scale=2.0)
        floor_of(floor_late, less_late, second_late)
        nc.vector.tensor_tensor(listed(wf, list4, s1, s2), largest[:, s1:s2], less_early[:, s1:s2], ALU.add)
        largest_of(largest[:, s2:], floor_late, first_late)
        nc.vector.tensor_tensor(listed(wf, list4, s2, I), largest[:, s2:], less_late, ALU.add)

        for lo, hi in zip(OUT_CUTS, OUT_CUTS[1:]):
            res = sb.tile([P, hi - lo], F32, name="res%d" % lo)
            nc.vector.scalar_tensor_tensor(res[:], old_sb[:, lo:hi], fade_sb[:], wf[:, lo:hi], ALU.mult, ALU.add)
            nc.sync.dma_start(out=out[:, lo:hi], in_=res[:])
